import numpy as np
import ml_dtypes


def mxq(x, axis, fmt="e4m3"):
    dtype, down = {"e4m3": (ml_dtypes.float8_e4m3fn, 7), "e5m2": (ml_dtypes.float8_e5m2, 14)}[fmt]
    v = np.moveaxis(np.asarray(x, np.float32).astype(ml_dtypes.bfloat16).astype(np.float64), axis, -1)
    blocks = v.reshape(v.shape[:-1] + (-1, 32))
    amax = np.abs(blocks).max(-1, keepdims=True)
    byte = np.maximum(np.where(amax > 0, np.frexp(amax)[1] - 1 + 127, 0) - down, 1)
    scale = np.exp2(byte - 127.0)
    codes = (blocks / scale).astype(np.float32).astype(dtype).astype(np.float64)
    return np.moveaxis((codes * scale).reshape(v.shape), -1, axis)


WIDE = False


def mx_kscale(k):
    if not WIDE:
        return np.ones(k)
    levels = np.array([10, -10, 5, -5, 0])
    if k % 512:
        return np.exp2(np.random.permutation(np.resize(levels, k // 32))).repeat(32)
    a = np.empty((k // 512, 16))
    for p in range(k // 512):
        a[p, :8] = np.random.permutation(np.resize(levels, 8))
        for g in range(8):
            far = levels[np.abs(levels - a[p, g]) >= 10]
            a[p, g + 8] = far[np.random.randint(len(far))]
    return np.exp2(a.ravel()).repeat(32)


def f64(x):
    return np.asarray(x).astype(np.float64)


def striped8(idx):
    return np.asarray(idx).reshape(8, -1, 16).transpose(0, 2, 1).reshape(128, -1).astype(np.uint16)


def unstriped8(offs):
    return offs.reshape(8, 16, -1).transpose(0, 2, 1).reshape(8, -1).astype(np.int64)


def pick8(x, idx, run):
    r = np.arange(len(x))
    return x[r[:, None], idx[r % (8 * run) // run]]


E2M1 = np.array([0.0, 0.5, 1.0, 1.5, 2.0, 3.0, 4.0, 6.0, -0.0, -0.5, -1.0, -1.5, -2.0, -3.0, -4.0, -6.0])


def pack_weight(w, fmt):
    k, n = w.shape
    w = f64(np.asarray(w, np.float32).astype(ml_dtypes.bfloat16)).reshape(k // 32, 32, n)
    amax = np.abs(w).max(1)
    if fmt == "e4m3":
        byte = np.frexp(amax)[1] - 1 + 127 - 7
    else:
        mant, ex = np.frexp(amax / 6.0)
        byte = np.where(mant > 0.5, ex, ex - 1) + 127
    byte = np.clip(np.where(amax > 0, byte, 1), 1, 254)
    scaled = (w * np.exp2(127.0 - byte)[:, None, :]).reshape(k, n).astype(np.float32)
    by_word = np.ascontiguousarray(scaled.reshape(k // 512, 128, 4, n).transpose(0, 1, 3, 2))
    if fmt == "e4m3":
        words = by_word.astype(ml_dtypes.float8_e4m3fn).view(np.uint8)
    else:
        c = by_word.astype(ml_dtypes.float4_e2m1fn).view(np.uint8) & 0xF
        words = (c[..., 0::2] | (c[..., 1::2] << 4)).reshape(k // 512, 128, 2 * n)
    return np.ascontiguousarray(words), np.ascontiguousarray(byte.astype(np.uint8).reshape(k // 512, 16, n))


def unpack_weight(words, scales, fmt):
    g, _, n = scales.shape
    words = np.ascontiguousarray(words).reshape(g, 128, n, -1)
    if fmt == "e4m3":
        vals = words.view(ml_dtypes.float8_e4m3fn).astype(np.float64)
    else:
        nib = np.empty((g, 128, n, 4), np.uint8)
        nib[..., 0::2] = words & 0xF
        nib[..., 1::2] = words >> 4
        vals = E2M1[nib]
    vals = vals * np.repeat(np.exp2(scales.astype(np.float64) - 127.0), 8, axis=1)[..., None]
    return vals.transpose(0, 1, 3, 2).reshape(g * 512, n)


D, K, T, U, X, I, J, Q = 512, 512, 1024, 1024, 1024, 512, 256, 128


def setup_inputs():
    n = np.random.standard_normal
    idx = np.stack([np.random.permutation(T)[:J] for _ in range(8)])
    idx2 = np.stack([np.random.permutation(U)[:J] for _ in range(8)])
    idx3 = np.stack([np.random.permutation(X)[:I] for _ in range(8)])
    idx4 = np.stack([np.random.permutation(X)[:I] for _ in range(8)])
    idx5 = np.stack([np.random.permutation(X)[:I] for _ in range(8)])
    fd = mx_kscale(D)
    fk = mx_kscale(K)
    wqp = pack_weight(n((D, K)) * 1.0 / np.sqrt(D) * fd[:, None] * fk, "e4m3")
    keysp = pack_weight(n((K, T)) * 1.0 / np.sqrt(K) / fk[:, None], "e4m3")
    notesp = pack_weight(n((K, U)) * 1.0 / np.sqrt(K) / fk[:, None], "e2m1")
    usersp = pack_weight(n((D, X)) * 1.0 / np.sqrt(D) * fd[:, None], "e4m3")
    return {
        "states": (n((D, Q)) * 0.95 / fd[:, None]).astype(np.float32),
        "wq_words": wqp[0],
        "wq_scales": wqp[1],
        "keys_words": keysp[0],
        "keys_scales": keysp[1],
        "notes_words": notesp[0],
        "notes_scales": notesp[1],
        "users_words": usersp[0],
        "users_scales": usersp[1],
        "offs": striped8(idx),
        "offs2": striped8(idx2),
        "offs3": striped8(idx3),
        "offs4": striped8(idx4),
        "offs5": striped8(idx5),
    }


def reference(states, wq_words, wq_scales, keys_words, keys_scales, notes_words, notes_scales, users_words, users_scales, offs, offs2, offs3, offs4, offs5):
    idx = unstriped8(offs)
    idx2 = unstriped8(offs2)
    idx3 = unstriped8(offs3)
    idx4 = unstriped8(offs4)
    idx5 = unstriped8(offs5)
    wqu = unpack_weight(wq_words, wq_scales, "e4m3")
    keysu = unpack_weight(keys_words, keys_scales, "e4m3")
    notesu = unpack_weight(notes_words, notes_scales, "e2m1")
    usersu = unpack_weight(users_words, users_scales, "e4m3")
    statesq = mxq(f64(states), 0, "e4m3")
    qv = wqu.T @ statesq
    qvq = mxq(qv, 0, "e4m3")
    a = qvq.T @ keysu
    b = qvq.T @ notesu
    c0 = statesq.T @ usersu
    w = np.concatenate([pick8(a, idx, 16), pick8(b, idx2, 16)], axis=1)
    v = np.maximum(w, pick8(c0, idx3, 16))
    f1 = np.zeros((Q, X))
    f1[np.arange(Q)[:, None], idx4[np.arange(Q) % 128 // 16]] = v
    cc = c0 + f1
    y = pick8(cc, idx5, 16)
    return y

@@ -1,0 +1,176 @@
+from contextlib import ExitStack
+
+import concourse.mybir as mybir
+
+F32 = mybir.dt.float32
+BF16 = mybir.dt.bfloat16
+I32 = mybir.dt.int32
+U32 = mybir.dt.uint32
+U16 = mybir.dt.uint16
+U8 = mybir.dt.uint8
+FP8X4 = mybir.dt.float8_e4m3fn_x4
+FP4X4 = mybir.dt.float4_e2m1fn_x4
+COPY = mybir.ActivationFunctionType.Copy
+ALU = mybir.AluOpType
+
+P = 128
+PACK = 4
+BANK = 512
+K = 512
+WIDE = 1024
+HALF = 256
+FLOPS = 2 * 512 * 128 * (512 + 3 * 1024)
+
+
+def tile_attend_joinedbest_madethree_kernel(
+    tc, states, wq_words, wq_scales, keys_words, keys_scales, notes_words, notes_scales,
+    users_words, users_scales, offs, offs2, offs3, offs4, offs5, out,
+):
+    nc = tc.nc
+    with ExitStack() as ctx:
+        sb = ctx.enter_context(tc.tile_pool(name="sb", bufs=1))
+        ps = ctx.enter_context(tc.psum_pool(name="ps", bufs=1))
+
+        def tile(shape, dtype, name):
+            return sb.tile(shape, dtype, name=name, align_bytes=64)
+
+        lists = {}
+        for name, cols in (("offs", 16), ("offs2", 16), ("offs3", 32), ("offs4", 32), ("offs5", 32)):
+            lists[name] = sb.tile([P, cols], U16, name="list_" + name)
+
+        states_raw = tile([P, PACK, P], F32, "states_raw")
+        states_bf = tile([P, P, PACK], BF16, "states_bf")
+        states_codes = tile([P, P], U32, "states_codes")
+        states_plane = tile([P, P], U8, "states_plane")
+        wq_raw = tile([P, K], U32, "wq_raw")
+        wq_dealt = tile([P, K], U32, "wq_dealt")
+        wq_plane_raw = tile([P, K], U8, "wq_plane_raw")
+        wq_plane = tile([P, K], U8, "wq_plane")
+        users_codes = tile([P, WIDE], U32, "users_codes")
+        users_plane = tile([P, WIDE], U8, "users_plane")
+        keys_codes = tile([P, WIDE], U32, "keys_codes")
+        keys_plane = tile([P, WIDE], U8, "keys_plane")
+        notes_codes = tile([P, 2 * WIDE], U8, "notes_codes")
+        notes_plane = tile([P, WIDE], U8, "notes_plane")
+        qv_bf = tile([P, P, PACK], BF16, "qv_bf")
+        qv_codes = tile([P, P], U32, "qv_codes")
+        qv_plane = tile([P, P], U8, "qv_plane")
+        a_sb = tile([P, WIDE], F32, "a_sb")
+        b_sb = tile([P, WIDE], F32, "b_sb")
+        c0_sb = tile([P, WIDE], F32, "c0_sb")
+        f1 = tile([P, WIDE], F32, "f1")
+        cc = tile([P, WIDE], F32, "cc")
+        w = [tile([P, HALF], F32, "w%d" % h) for h in range(2)]
+        g = [tile([P, HALF], F32, "g%d" % h) for h in range(2)]
+        v = [tile([P, HALF], F32, "v%d" % h) for h in range(2)]
+        y = [tile([P, HALF], F32, "y%d" % h) for h in range(2)]
+
+        qv_ps = ps.tile([P, PACK, P], F32, name="qv_ps")
+        c0_ps = [ps.tile([P, BANK], F32, name="c0_ps%d" % n) for n in range(2)]
+        a_ps = [ps.tile([P, BANK], F32, name="a_ps%d" % n) for n in range(2)]
+        b_ps = [ps.tile([P, BANK], F32, name="b_ps%d" % n) for n in range(2)]
+
+        def load_words(dst, src):
+            nc.sync.dma_start(out=dst[:].bitcast(I32), in_=src.bitcast(I32))
+
+        def load_plane(queue, dst, src):
+            for quad in range(4):
+                queue.dma_start(
+                    out=dst[32 * quad : 32 * quad + 4, :].bitcast(I32),
+                    in_=src[0, 4 * quad : 4 * quad + 4, :].bitcast(I32),
+                )
+
+        def load_list(name, src):
+            nc.sync.dma_start(lists[name][:], src)
+
+        nc.vector.memset(wq_plane_raw[:].bitcast(U32), 0)
+        nc.gpsimd.memset(users_plane[:].bitcast(U32), 0)
+        nc.vector.memset(keys_plane[:].bitcast(U32), 0)
+        nc.gpsimd.memset(notes_plane[:].bitcast(U32), 0)
+        nc.vector.memset(f1[:], 0.0)
+
+        nc.sync.dma_start(out=states_raw[:], in_=states.rearrange("(p j) q -> p j q", j=PACK))
+        load_words(wq_raw, wq_words[0].rearrange("p n t -> p (n t)"))
+        load_plane(nc.scalar, wq_plane_raw, wq_scales)
+        load_words(users_codes, users_words[0].rearrange("p n t -> p (n t)"))
+        load_plane(nc.sync, users_plane, users_scales)
+        load_words(keys_codes, keys_words[0].rearrange("p n t -> p (n t)"))
+        load_plane(nc.sync, keys_plane, keys_scales)
+        load_list("offs3", offs3)
+        load_words(notes_codes, notes_words[0])
+        load_plane(nc.sync, notes_plane, notes_scales)
+        load_list("offs", offs)
+        load_list("offs4", offs4)
+        load_list("offs2", offs2)
+        load_list("offs5", offs5)
+
+        nc.vector.tensor_copy(
+            out=wq_plane[:].rearrange("p (j m) -> p j m", j=PACK),
+            in_=wq_plane_raw[:].rearrange("p (m j) -> p j m", j=PACK),
+        )
+        nc.vector.tensor_copy(
+            out=states_bf[:].rearrange("p (c i) j -> p c j i", i=4),
+            in_=states_raw[:].rearrange("p j (c i) -> p c j i", i=4),
+        )
+        nc.scalar.copy(
+            out=wq_dealt[:].rearrange("p (j c i) -> p c j i", j=PACK, i=4),
+            in_=wq_raw[:].rearrange("p (c i j) -> p c j i", j=PACK, i=4),
+        )
+        nc.vector.quantize_mx(
+            out=states_codes[:].bitcast(FP8X4), scales=states_plane[:],
+            in_=states_bf[:].rearrange("p q j -> p (q j)"),
+        )
+
+        for j in range(PACK):
+            cols = slice(j * P, (j + 1) * P)
+            nc.tensor.matmul_mx(
+                out=qv_ps[:, j, :], lhsT=wq_dealt[:, cols].bitcast(FP8X4), lhsT_scale=wq_plane[:, cols],
+                rhs=states_codes[:].bitcast(FP8X4), rhs_scale=states_plane[:], start=True, stop=True,
+            )
+
+        def scores(banks, codes, plane, moving, moving_plane):
+            for n in range(2):
+                nc.tensor.matmul_mx(
+                    out=banks[n][:], lhsT=codes[:].bitcast(FP8X4), lhsT_scale=plane[:],
+                    rhs=moving(n), rhs_scale=moving_plane[:, n * BANK : (n + 1) * BANK],
+                    start=True, stop=True,
+                )
+
+        scores(c0_ps, states_codes, states_plane,
+               lambda n: users_codes[:, n * BANK : (n + 1) * BANK].bitcast(FP8X4), users_plane)
+
+        nc.vector.tensor_copy(out=qv_bf[:], in_=qv_ps[:].rearrange("p j q -> p q j"))
+        nc.vector.quantize_mx(
+            out=qv_codes[:].bitcast(FP8X4), scales=qv_plane[:],
+            in_=qv_bf[:].rearrange("p q j -> p (q j)"),
+        )
+        scores(a_ps, qv_codes, qv_plane,
+               lambda n: keys_codes[:, n * BANK : (n + 1) * BANK].bitcast(FP8X4), keys_plane)
+        scores(b_ps, qv_codes, qv_plane,
+               lambda n: notes_codes[:, 2 * n * BANK : 2 * (n + 1) * BANK].bitcast(FP4X4), notes_plane)
+
+        def half(name, h):
+            return lists[name][:, 16 * h : 16 * (h + 1)]
+
+        nc.scalar.copy(out=c0_sb[:, :BANK], in_=c0_ps[0][:])
+        nc.scalar.copy(out=c0_sb[:, BANK:], in_=c0_ps[1][:])
+        nc.scalar.activation(g[0][:], c0_sb[:].indirect(half("offs3", 0)), COPY)
+
+        nc.vector.tensor_copy(out=a_sb[:, :BANK], in_=a_ps[0][:])
+        nc.scalar.copy(out=a_sb[:, BANK:], in_=a_ps[1][:])
+        nc.vector.tensor_copy(w[0][:], a_sb[:].indirect(lists["offs"][:]))
+        nc.vector.tensor_tensor(v[0][:], w[0][:], g[0][:], ALU.max)
+        nc.vector.tensor_copy(f1[:].indirect(half("offs4", 0)), v[0][:])
+
+        nc.scalar.copy(out=b_sb[:, :BANK], in_=b_ps[0][:])
+        nc.scalar.copy(out=b_sb[:, BANK:], in_=b_ps[1][:])
+        nc.scalar.activation(w[1][:], b_sb[:].indirect(lists["offs2"][:]), COPY)
+        nc.scalar.activation(g[1][:], c0_sb[:].indirect(half("offs3", 1)), COPY)
+        nc.vector.tensor_tensor(v[1][:], w[1][:], g[1][:], ALU.max)
+        nc.vector.tensor_copy(f1[:].indirect(half("offs4", 1)), v[1][:])
+
+        nc.vector.tensor_tensor(cc[:], c0_sb[:], f1[:], ALU.add)
+        nc.vector.tensor_copy(y[0][:], cc[:].indirect(half("offs5", 0)))
+        nc.scalar.activation(y[1][:], cc[:].indirect(half("offs5", 1)), COPY)
+        nc.sync.dma_start(out=out[:, :HALF], in_=y[0][:])
+        nc.scalar.dma_start(out=out[:, HALF:], in_=y[1][:])

@@ -43,9 +43,9 @@ def tile_attend_joinedbest_madethree_kernel(
         states_codes = tile([P, P], U32, "states_codes")
         states_plane = tile([P, P], U8, "states_plane")
         wq_raw = tile([P, K], U32, "wq_raw")
-        wq_dealt = tile([P, K], U32, "wq_dealt")
+        wq_dealt = [tile([P, P], U32, "wq_dealt%d" % j) for j in range(PACK)]
         wq_plane_raw = tile([P, K], U8, "wq_plane_raw")
-        wq_plane = tile([P, K], U8, "wq_plane")
+        wq_plane = [tile([P, P], U8, "wq_plane%d" % j) for j in range(PACK)]
         users_codes = tile([P, WIDE], U32, "users_codes")
         users_plane = tile([P, WIDE], U8, "users_plane")
         keys_codes = tile([P, WIDE], U32, "keys_codes")
@@ -61,7 +61,7 @@ def tile_attend_joinedbest_madethree_kernel(
         f1 = tile([P, WIDE], F32, "f1")
         cc = tile([P, WIDE], F32, "cc")
         w = [tile([P, HALF], F32, "w%d" % h) for h in range(2)]
-        g = [tile([P, HALF], F32, "g%d" % h) for h in range(2)]
+        g = tile([P, 2 * HALF], F32, "g")
         v = [tile([P, HALF], F32, "v%d" % h) for h in range(2)]
         y = [tile([P, HALF], F32, "y%d" % h) for h in range(2)]
 
@@ -73,8 +73,8 @@ def tile_attend_joinedbest_madethree_kernel(
         def load_words(dst, src):
             nc.sync.dma_start(out=dst[:].bitcast(I32), in_=src.bitcast(I32))
 
-        def load_plane(queue, dst, src):
-            for quad in range(4):
+        def load_plane(queue, dst, src, quads=range(4)):
+            for quad in quads:
                 queue.dma_start(
                     out=dst[32 * quad : 32 * quad + 4, :].bitcast(I32),
                     in_=src[0, 4 * quad : 4 * quad + 4, :].bitcast(I32),
@@ -84,37 +84,31 @@ def tile_attend_joinedbest_madethree_kernel(
             nc.sync.dma_start(lists[name][:], src)
 
         nc.vector.memset(wq_plane_raw[:].bitcast(U32), 0)
-        nc.gpsimd.memset(users_plane[:].bitcast(U32), 0)
-        nc.vector.memset(keys_plane[:].bitcast(U32), 0)
-        nc.gpsimd.memset(notes_plane[:].bitcast(U32), 0)
+        nc.gpsimd.memset(keys_plane[:].bitcast(U32), 0)
+        nc.vector.memset(users_plane[:].bitcast(U32), 0)
+        nc.vector.memset(notes_plane[:].bitcast(U32), 0)
         nc.vector.memset(f1[:], 0.0)
 
         nc.sync.dma_start(out=states_raw[:], in_=states.rearrange("(p j) q -> p j q", j=PACK))
+        load_plane(nc.sync, wq_plane_raw, wq_scales)
         load_words(wq_raw, wq_words[0].rearrange("p n t -> p (n t)"))
-        load_plane(nc.scalar, wq_plane_raw, wq_scales)
         load_words(users_codes, users_words[0].rearrange("p n t -> p (n t)"))
         load_plane(nc.sync, users_plane, users_scales)
         load_words(keys_codes, keys_words[0].rearrange("p n t -> p (n t)"))
-        load_plane(nc.sync, keys_plane, keys_scales)
+        load_plane(nc.sync, keys_plane, keys_scales, (0, 1))
+        load_plane(nc.gpsimd, keys_plane, keys_scales, (2, 3))
         load_list("offs3", offs3)
         load_words(notes_codes, notes_words[0])
-        load_plane(nc.sync, notes_plane, notes_scales)
         load_list("offs", offs)
+        load_plane(nc.sync, notes_plane, notes_scales, (0, 1))
+        load_plane(nc.gpsimd, notes_plane, notes_scales, (2, 3))
         load_list("offs4", offs4)
         load_list("offs2", offs2)
         load_list("offs5", offs5)
 
         nc.vector.tensor_copy(
-            out=wq_plane[:].rearrange("p (j m) -> p j m", j=PACK),
-            in_=wq_plane_raw[:].rearrange("p (m j) -> p j m", j=PACK),
-        )
-        nc.vector.tensor_copy(
             out=states_bf[:].rearrange("p (c i) j -> p c j i", i=4),
             in_=states_raw[:].rearrange("p j (c i) -> p c j i", i=4),
-        )
-        nc.scalar.copy(
-            out=wq_dealt[:].rearrange("p (j c i) -> p c j i", j=PACK, i=4),
-            in_=wq_raw[:].rearrange("p (c i j) -> p c j i", j=PACK, i=4),
         )
         nc.vector.quantize_mx(
             out=states_codes[:].bitcast(FP8X4), scales=states_plane[:],
@@ -122,51 +116,54 @@ def tile_attend_joinedbest_madethree_kernel(
         )
 
         for j in range(PACK):
-            cols = slice(j * P, (j + 1) * P)
+            nc.vector.tensor_copy(out=wq_plane[j][:], in_=wq_plane_raw[:, j::PACK])
+            nc.scalar.copy(out=wq_dealt[j][:], in_=wq_raw[:, j::PACK])
             nc.tensor.matmul_mx(
-                out=qv_ps[:, j, :], lhsT=wq_dealt[:, cols].bitcast(FP8X4), lhsT_scale=wq_plane[:, cols],
+                out=qv_ps[:, j, :], lhsT=wq_dealt[j][:].bitcast(FP8X4), lhsT_scale=wq_plane[j][:],
                 rhs=states_codes[:].bitcast(FP8X4), rhs_scale=states_plane[:], start=True, stop=True,
             )
 
         def scores(banks, codes, plane, moving, moving_plane):
-            for n in range(2):
+            lo = 0
+            for bank in banks:
+                hi = lo + bank.shape[1]
                 nc.tensor.matmul_mx(
-                    out=banks[n][:], lhsT=codes[:].bitcast(FP8X4), lhsT_scale=plane[:],
-                    rhs=moving(n), rhs_scale=moving_plane[:, n * BANK : (n + 1) * BANK],
+                    out=bank[:], lhsT=codes[:].bitcast(FP8X4), lhsT_scale=plane[:],
+                    rhs=moving(lo, hi), rhs_scale=moving_plane[:, lo:hi],
                     start=True, stop=True,
                 )
+                lo = hi
 
         scores(c0_ps, states_codes, states_plane,
-               lambda n: users_codes[:, n * BANK : (n + 1) * BANK].bitcast(FP8X4), users_plane)
+               lambda lo, hi: users_codes[:, lo:hi].bitcast(FP8X4), users_plane)
 
-        nc.vector.tensor_copy(out=qv_bf[:], in_=qv_ps[:].rearrange("p j q -> p q j"))
+        nc.scalar.copy(out=qv_bf[:], in_=qv_ps[:].rearrange("p j q -> p q j"))
         nc.vector.quantize_mx(
             out=qv_codes[:].bitcast(FP8X4), scales=qv_plane[:],
             in_=qv_bf[:].rearrange("p q j -> p (q j)"),
         )
         scores(a_ps, qv_codes, qv_plane,
-               lambda n: keys_codes[:, n * BANK : (n + 1) * BANK].bitcast(FP8X4), keys_plane)
+               lambda lo, hi: keys_codes[:, lo:hi].bitcast(FP8X4), keys_plane)
         scores(b_ps, qv_codes, qv_plane,
-               lambda n: notes_codes[:, 2 * n * BANK : 2 * (n + 1) * BANK].bitcast(FP4X4), notes_plane)
+               lambda lo, hi: notes_codes[:, 2 * lo : 2 * hi].bitcast(FP4X4), notes_plane)
 
         def half(name, h):
             return lists[name][:, 16 * h : 16 * (h + 1)]
 
         nc.scalar.copy(out=c0_sb[:, :BANK], in_=c0_ps[0][:])
-        nc.scalar.copy(out=c0_sb[:, BANK:], in_=c0_ps[1][:])
-        nc.scalar.activation(g[0][:], c0_sb[:].indirect(half("offs3", 0)), COPY)
+        nc.vector.tensor_copy(out=c0_sb[:, BANK:], in_=c0_ps[1][:])
+        nc.scalar.activation(g[:], c0_sb[:].indirect(lists["offs3"][:]), COPY)
 
         nc.vector.tensor_copy(out=a_sb[:, :BANK], in_=a_ps[0][:])
-        nc.scalar.copy(out=a_sb[:, BANK:], in_=a_ps[1][:])
+        nc.vector.tensor_copy(out=a_sb[:, BANK:], in_=a_ps[1][:])
         nc.vector.tensor_copy(w[0][:], a_sb[:].indirect(lists["offs"][:]))
-        nc.vector.tensor_tensor(v[0][:], w[0][:], g[0][:], ALU.max)
+        nc.vector.tensor_tensor(v[0][:], w[0][:], g[:, :HALF], ALU.max)
         nc.vector.tensor_copy(f1[:].indirect(half("offs4", 0)), v[0][:])
 
         nc.scalar.copy(out=b_sb[:, :BANK], in_=b_ps[0][:])
         nc.scalar.copy(out=b_sb[:, BANK:], in_=b_ps[1][:])
         nc.scalar.activation(w[1][:], b_sb[:].indirect(lists["offs2"][:]), COPY)
-        nc.scalar.activation(g[1][:], c0_sb[:].indirect(half("offs3", 1)), COPY)
-        nc.vector.tensor_tensor(v[1][:], w[1][:], g[1][:], ALU.max)
+        nc.vector.tensor_tensor(v[1][:], w[1][:], g[:, HALF:], ALU.max)
         nc.vector.tensor_copy(f1[:].indirect(half("offs4", 1)), v[1][:])
 
         nc.vector.tensor_tensor(cc[:], c0_sb[:], f1[:], ALU.add)

@@ -19,6 +19,7 @@ BANK = 512
 K = 512
 WIDE = 1024
 HALF = 256
+CUT = 736
 FLOPS = 2 * 512 * 128 * (512 + 3 * 1024)
 
 
@@ -43,9 +44,9 @@ def tile_attend_joinedbest_madethree_kernel(
         states_codes = tile([P, P], U32, "states_codes")
         states_plane = tile([P, P], U8, "states_plane")
         wq_raw = tile([P, K], U32, "wq_raw")
-        wq_dealt = [tile([P, P], U32, "wq_dealt%d" % j) for j in range(PACK)]
+        wq_dealt = [tile([P, 2 * P], U32, "wq_dealt%d" % pair) for pair in range(2)]
         wq_plane_raw = tile([P, K], U8, "wq_plane_raw")
-        wq_plane = [tile([P, P], U8, "wq_plane%d" % j) for j in range(PACK)]
+        wq_plane = tile([P, K], U8, "wq_plane")
         users_codes = tile([P, WIDE], U32, "users_codes")
         users_plane = tile([P, WIDE], U8, "users_plane")
         keys_codes = tile([P, WIDE], U32, "keys_codes")
@@ -60,14 +61,14 @@ def tile_attend_joinedbest_madethree_kernel(
         c0_sb = tile([P, WIDE], F32, "c0_sb")
         f1 = tile([P, WIDE], F32, "f1")
         cc = tile([P, WIDE], F32, "cc")
-        w = [tile([P, HALF], F32, "w%d" % h) for h in range(2)]
-        g = tile([P, 2 * HALF], F32, "g")
+        w = tile([P, HALF], F32, "w")
+        g = [tile([P, HALF], F32, "g%d" % h) for h in range(2)]
         v = [tile([P, HALF], F32, "v%d" % h) for h in range(2)]
         y = [tile([P, HALF], F32, "y%d" % h) for h in range(2)]
 
-        qv_ps = ps.tile([P, PACK, P], F32, name="qv_ps")
+        qv_ps = ps.tile([P, PACK, P], F32, name="qv_ps", tag="qv_bank")
         c0_ps = [ps.tile([P, BANK], F32, name="c0_ps%d" % n) for n in range(2)]
-        a_ps = [ps.tile([P, BANK], F32, name="a_ps%d" % n) for n in range(2)]
+        a_ps = [ps.tile([P, HALF], F32, name="a_ps%d" % n) for n in range(3)]
         b_ps = [ps.tile([P, BANK], F32, name="b_ps%d" % n) for n in range(2)]
 
         def load_words(dst, src):
@@ -106,20 +107,30 @@ def tile_attend_joinedbest_madethree_kernel(
         load_list("offs2", offs2)
         load_list("offs5", offs5)
 
+        for copy, rows in ((nc.vector.tensor_copy, slice(0, P // 2)), (nc.scalar.copy, slice(P // 2, P))):
+            copy(
+                out=states_bf[:, rows, :].rearrange("p (c i) j -> p c j i", i=4),
+                in_=states_raw[:, :, rows].rearrange("p j (c i) -> p c j i", i=4),
+            )
         nc.vector.tensor_copy(
-            out=states_bf[:].rearrange("p (c i) j -> p c j i", i=4),
-            in_=states_raw[:].rearrange("p j (c i) -> p c j i", i=4),
+            out=wq_plane[:].rearrange("p (j m) -> p j m", j=PACK),
+            in_=wq_plane_raw[:].rearrange("p (m j) -> p j m", j=PACK),
         )
         nc.vector.quantize_mx(
             out=states_codes[:].bitcast(FP8X4), scales=states_plane[:],
             in_=states_bf[:].rearrange("p q j -> p (q j)"),
         )
+        for pair, (copy, word) in enumerate(((nc.scalar.copy, U32), (nc.vector.tensor_copy, I32))):
+            copy(
+                out=wq_dealt[pair][:].bitcast(word).rearrange("p (j c i) -> p c j i", j=2, i=4),
+                in_=wq_raw[:].bitcast(word).rearrange("p (c i j) -> p c j i", i=4, j=PACK)[:, :, 2 * pair : 2 * pair + 2, :],
+            )
 
         for j in range(PACK):
-            nc.vector.tensor_copy(out=wq_plane[j][:], in_=wq_plane_raw[:, j::PACK])
-            nc.scalar.copy(out=wq_dealt[j][:], in_=wq_raw[:, j::PACK])
             nc.tensor.matmul_mx(
-                out=qv_ps[:, j, :], lhsT=wq_dealt[j][:].bitcast(FP8X4), lhsT_scale=wq_plane[j][:],
+                out=qv_ps[:, j, :],
+                lhsT=wq_dealt[j // 2][:, j % 2 * P : (j % 2 + 1) * P].bitcast(FP8X4),
+                lhsT_scale=wq_plane[:, j * P : (j + 1) * P],
                 rhs=states_codes[:].bitcast(FP8X4), rhs_scale=states_plane[:], start=True, stop=True,
             )
 
@@ -137,11 +148,12 @@ def tile_attend_joinedbest_madethree_kernel(
         scores(c0_ps, states_codes, states_plane,
                lambda lo, hi: users_codes[:, lo:hi].bitcast(FP8X4), users_plane)
 
-        nc.scalar.copy(out=qv_bf[:], in_=qv_ps[:].rearrange("p j q -> p q j"))
+        nc.vector.tensor_copy(out=qv_bf[:], in_=qv_ps[:].rearrange("p j q -> p q j"))
         nc.vector.quantize_mx(
             out=qv_codes[:].bitcast(FP8X4), scales=qv_plane[:],
             in_=qv_bf[:].rearrange("p q j -> p (q j)"),
         )
+        a_ps.append(ps.tile([P, HALF], F32, name="a_ps3", tag="qv_bank"))
         scores(a_ps, qv_codes, qv_plane,
                lambda lo, hi: keys_codes[:, lo:hi].bitcast(FP8X4), keys_plane)
         scores(b_ps, qv_codes, qv_plane,
@@ -151,22 +163,25 @@ def tile_attend_joinedbest_madethree_kernel(
             return lists[name][:, 16 * h : 16 * (h + 1)]
 
         nc.scalar.copy(out=c0_sb[:, :BANK], in_=c0_ps[0][:])
-        nc.vector.tensor_copy(out=c0_sb[:, BANK:], in_=c0_ps[1][:])
-        nc.scalar.activation(g[:], c0_sb[:].indirect(lists["offs3"][:]), COPY)
+        nc.scalar.copy(out=c0_sb[:, BANK:], in_=c0_ps[1][:])
+        for h in range(2):
+            nc.scalar.activation(g[h][:], c0_sb[:].indirect(half("offs3", h)), COPY)
 
-        nc.vector.tensor_copy(out=a_sb[:, :BANK], in_=a_ps[0][:])
-        nc.vector.tensor_copy(out=a_sb[:, BANK:], in_=a_ps[1][:])
-        nc.vector.tensor_copy(w[0][:], a_sb[:].indirect(lists["offs"][:]))
-        nc.vector.tensor_tensor(v[0][:], w[0][:], g[:, :HALF], ALU.max)
+        for n in range(4):
+            nc.vector.tensor_copy(out=a_sb[:, n * HALF : (n + 1) * HALF], in_=a_ps[n][:])
+        nc.vector.tensor_copy(w[:], a_sb[:].indirect(lists["offs"][:]))
+        nc.vector.tensor_tensor(v[0][:], w[:], g[0][:], ALU.max)
         nc.vector.tensor_copy(f1[:].indirect(half("offs4", 0)), v[0][:])
 
         nc.scalar.copy(out=b_sb[:, :BANK], in_=b_ps[0][:])
         nc.scalar.copy(out=b_sb[:, BANK:], in_=b_ps[1][:])
-        nc.scalar.activation(w[1][:], b_sb[:].indirect(lists["offs2"][:]), COPY)
-        nc.vector.tensor_tensor(v[1][:], w[1][:], g[:, HALF:], ALU.max)
+        nc.scalar.activation(w[:], b_sb[:].indirect(lists["offs2"][:]), COPY)
+        nc.vector.tensor_tensor(v[1][:], w[:], g[1][:], ALU.max)
         nc.vector.tensor_copy(f1[:].indirect(half("offs4", 1)), v[1][:])
 
-        nc.vector.tensor_tensor(cc[:], c0_sb[:], f1[:], ALU.add)
+        nc.vector.tensor_tensor(cc[:, :BANK], f1[:, :BANK], c0_ps[0][:], ALU.add)
+        nc.vector.tensor_tensor(cc[:, BANK:CUT], f1[:, BANK:CUT], c0_ps[1][:, : CUT - BANK], ALU.add)
+        nc.gpsimd.tensor_tensor(cc[:, CUT:], f1[:, CUT:], c0_sb[:, CUT:], ALU.add)
         nc.vector.tensor_copy(y[0][:], cc[:].indirect(half("offs5", 0)))
         nc.scalar.activation(y[1][:], cc[:].indirect(half("offs5", 1)), COPY)
         nc.sync.dma_start(out=out[:, :HALF], in_=y[0][:])

from contextlib import ExitStack

import concourse.mybir as mybir

F32 = mybir.dt.float32
BF16 = mybir.dt.bfloat16
I32 = mybir.dt.int32
U32 = mybir.dt.uint32
U16 = mybir.dt.uint16
U8 = mybir.dt.uint8
FP8X4 = mybir.dt.float8_e4m3fn_x4
FP4X4 = mybir.dt.float4_e2m1fn_x4
COPY = mybir.ActivationFunctionType.Copy
ALU = mybir.AluOpType

P = 128
PACK = 4
BANK = 512
K = 512
WIDE = 1024
HALF = 256
CUT = 736
FLOPS = 2 * 512 * 128 * (512 + 3 * 1024)


def tile_attend_joinedbest_madethree_kernel(
    tc, states, wq_words, wq_scales, keys_words, keys_scales, notes_words, notes_scales,
    users_words, users_scales, offs, offs2, offs3, offs4, offs5, out,
):
    nc = tc.nc
    with ExitStack() as ctx:
        sb = ctx.enter_context(tc.tile_pool(name="sb", bufs=1))
        ps = ctx.enter_context(tc.psum_pool(name="ps", bufs=1))

        def tile(shape, dtype, name):
            return sb.tile(shape, dtype, name=name, align_bytes=64)

        lists = {}
        for name, cols in (("offs", 16), ("offs2", 16), ("offs3", 32), ("offs4", 32), ("offs5", 32)):
            lists[name] = sb.tile([P, cols], U16, name="list_" + name)

        states_raw = tile([P, PACK, P], F32, "states_raw")
        states_bf = tile([P, P, PACK], BF16, "states_bf")
        states_codes = tile([P, P], U32, "states_codes")
        states_plane = tile([P, P], U8, "states_plane")
        wq_raw = tile([P, K], U32, "wq_raw")
        wq_dealt = [tile([P, 2 * P], U32, "wq_dealt%d" % pair) for pair in range(2)]
        wq_plane_raw = tile([P, K], U8, "wq_plane_raw")
        wq_plane = tile([P, K], U8, "wq_plane")
        users_codes = tile([P, WIDE], U32, "users_codes")
        users_plane = tile([P, WIDE], U8, "users_plane")
        keys_codes = tile([P, WIDE], U32, "keys_codes")
        keys_plane = tile([P, WIDE], U8, "keys_plane")
        notes_codes = tile([P, 2 * WIDE], U8, "notes_codes")
        notes_plane = tile([P, WIDE], U8, "notes_plane")
        qv_bf = tile([P, P, PACK], BF16, "qv_bf")
        qv_codes = tile([P, P], U32, "qv_codes")
        qv_plane = tile([P, P], U8, "qv_plane")
        a_sb = tile([P, WIDE], F32, "a_sb")
        b_sb = tile([P, WIDE], F32, "b_sb")
        c0_sb = tile([P, WIDE], F32, "c0_sb")
        f1 = tile([P, WIDE], F32, "f1")
        cc = tile([P, WIDE], F32, "cc")
        w = tile([P, HALF], F32, "w")
        g = [tile([P, HALF], F32, "g%d" % h) for h in range(2)]
        v = [tile([P, HALF], F32, "v%d" % h) for h in range(2)]
        y = [tile([P, HALF], F32, "y%d" % h) for h in range(2)]

        qv_ps = ps.tile([P, PACK, P], F32, name="qv_ps", tag="qv_bank")
        c0_ps = [ps.tile([P, BANK], F32, name="c0_ps%d" % n) for n in range(2)]
        a_ps = [ps.tile([P, HALF], F32, name="a_ps%d" % n) for n in range(3)]
        b_ps = [ps.tile([P, BANK], F32, name="b_ps%d" % n) for n in range(2)]

        def load_words(dst, src):
            nc.sync.dma_start(out=dst[:].bitcast(I32), in_=src.bitcast(I32))

        def load_plane(queue, dst, src, quads=range(4)):
            for quad in quads:
                queue.dma_start(
                    out=dst[32 * quad : 32 * quad + 4, :].bitcast(I32),
                    in_=src[0, 4 * quad : 4 * quad + 4, :].bitcast(I32),
                )

        def load_list(name, src):
            nc.sync.dma_start(lists[name][:], src)

        nc.vector.memset(wq_plane_raw[:].bitcast(U32), 0)
        nc.gpsimd.memset(keys_plane[:].bitcast(U32), 0)
        nc.vector.memset(users_plane[:].bitcast(U32), 0)
        nc.vector.memset(notes_plane[:].bitcast(U32), 0)
        nc.vector.memset(f1[:], 0.0)

        nc.sync.dma_start(out=states_raw[:], in_=states.rearrange("(p j) q -> p j q", j=PACK))
        load_plane(nc.sync, wq_plane_raw, wq_scales)
        load_words(wq_raw, wq_words[0].rearrange("p n t -> p (n t)"))
        load_words(users_codes, users_words[0].rearrange("p n t -> p (n t)"))
        load_plane(nc.sync, users_plane, users_scales)
        load_words(keys_codes, keys_words[0].rearrange("p n t -> p (n t)"))
        load_plane(nc.sync, keys_plane, keys_scales, (0, 1))
        load_plane(nc.gpsimd, keys_plane, keys_scales, (2, 3))
        load_list("offs3", offs3)
        load_words(notes_codes, notes_words[0])
        load_list("offs", offs)
        load_plane(nc.sync, notes_plane, notes_scales, (0, 1))
        load_plane(nc.gpsimd, notes_plane, notes_scales, (2, 3))
        load_list("offs4", offs4)
        load_list("offs2", offs2)
        load_list("offs5", offs5)

        for copy, rows in ((nc.vector.tensor_copy, slice(0, P // 2)), (nc.scalar.copy, slice(P // 2, P))):
            copy(
                out=states_bf[:, rows, :].rearrange("p (c i) j -> p c j i", i=4),
                in_=states_raw[:, :, rows].rearrange("p j (c i) -> p c j i", i=4),
            )
        nc.vector.tensor_copy(
            out=wq_plane[:].rearrange("p (j m) -> p j m", j=PACK),
            in_=wq_plane_raw[:].rearrange("p (m j) -> p j m", j=PACK),
        )
        nc.vector.quantize_mx(
            out=states_codes[:].bitcast(FP8X4), scales=states_plane[:],
            in_=states_bf[:].rearrange("p q j -> p (q j)"),
        )
        for pair, (copy, word) in enumerate(((nc.scalar.copy, U32), (nc.vector.tensor_copy, I32))):
            copy(
                out=wq_dealt[pair][:].bitcast(word).rearrange("p (j c i) -> p c j i", j=2, i=4),
                in_=wq_raw[:].bitcast(word).rearrange("p (c i j) -> p c j i", i=4, j=PACK)[:, :, 2 * pair : 2 * pair + 2, :],
            )

        for j in range(PACK):
            nc.tensor.matmul_mx(
                out=qv_ps[:, j, :],
                lhsT=wq_dealt[j // 2][:, j % 2 * P : (j % 2 + 1) * P].bitcast(FP8X4),
                lhsT_scale=wq_plane[:, j * P : (j + 1) * P],
                rhs=states_codes[:].bitcast(FP8X4), rhs_scale=states_plane[:], start=True, stop=True,
            )

        def scores(banks, codes, plane, moving, moving_plane):
            lo = 0
            for bank in banks:
                hi = lo + bank.shape[1]
                nc.tensor.matmul_mx(
                    out=bank[:], lhsT=codes[:].bitcast(FP8X4), lhsT_scale=plane[:],
                    rhs=moving(lo, hi), rhs_scale=moving_plane[:, lo:hi],
                    start=True, stop=True,
                )
                lo = hi

        scores(c0_ps, states_codes, states_plane,
               lambda lo, hi: users_codes[:, lo:hi].bitcast(FP8X4), users_plane)

        nc.vector.tensor_copy(out=qv_bf[:], in_=qv_ps[:].rearrange("p j q -> p q j"))
        nc.vector.quantize_mx(
            out=qv_codes[:].bitcast(FP8X4), scales=qv_plane[:],
            in_=qv_bf[:].rearrange("p q j -> p (q j)"),
        )
        a_ps.append(ps.tile([P, HALF], F32, name="a_ps3", tag="qv_bank"))
        scores(a_ps, qv_codes, qv_plane,
               lambda lo, hi: keys_codes[:, lo:hi].bitcast(FP8X4), keys_plane)
        scores(b_ps, qv_codes, qv_plane,
               lambda lo, hi: notes_codes[:, 2 * lo : 2 * hi].bitcast(FP4X4), notes_plane)

        def half(name, h):
            return lists[name][:, 16 * h : 16 * (h + 1)]

        nc.scalar.copy(out=c0_sb[:, :BANK], in_=c0_ps[0][:])
        nc.scalar.copy(out=c0_sb[:, BANK:], in_=c0_ps[1][:])
        for h in range(2):
            nc.scalar.activation(g[h][:], c0_sb[:].indirect(half("offs3", h)), COPY)

        for n in range(4):
            nc.vector.tensor_copy(out=a_sb[:, n * HALF : (n + 1) * HALF], in_=a_ps[n][:])
        nc.vector.tensor_copy(w[:], a_sb[:].indirect(lists["offs"][:]))
        nc.vector.tensor_tensor(v[0][:], w[:], g[0][:], ALU.max)
        nc.vector.tensor_copy(f1[:].indirect(half("offs4", 0)), v[0][:])

        nc.scalar.copy(out=b_sb[:, :BANK], in_=b_ps[0][:])
        nc.scalar.copy(out=b_sb[:, BANK:], in_=b_ps[1][:])
        nc.scalar.activation(w[:], b_sb[:].indirect(lists["offs2"][:]), COPY)
        nc.vector.tensor_tensor(v[1][:], w[:], g[1][:], ALU.max)
        nc.vector.tensor_copy(f1[:].indirect(half("offs4", 1)), v[1][:])

        nc.vector.tensor_tensor(cc[:, :BANK], f1[:, :BANK], c0_ps[0][:], ALU.add)
        nc.vector.tensor_tensor(cc[:, BANK:CUT], f1[:, BANK:CUT], c0_ps[1][:, : CUT - BANK], ALU.add)
        nc.gpsimd.tensor_tensor(cc[:, CUT:], f1[:, CUT:], c0_sb[:, CUT:], ALU.add)
        nc.vector.tensor_copy(y[0][:], cc[:].indirect(half("offs5", 0)))
        nc.scalar.activation(y[1][:], cc[:].indirect(half("offs5", 1)), COPY)
        nc.sync.dma_start(out=out[:, :HALF], in_=y[0][:])
        nc.scalar.dma_start(out=out[:, HALF:], in_=y[1][:])
